import numpy as np
import ml_dtypes


def mxq(x, axis, fmt="e4m3"):
    dtype, down = {"e4m3": (ml_dtypes.float8_e4m3fn, 7), "e5m2": (ml_dtypes.float8_e5m2, 14)}[fmt]
    v = np.moveaxis(np.asarray(x, np.float32).astype(ml_dtypes.bfloat16).astype(np.float64), axis, -1)
    blocks = v.reshape(v.shape[:-1] + (-1, 32))
    amax = np.abs(blocks).max(-1, keepdims=True)
    byte = np.maximum(np.where(amax > 0, np.frexp(amax)[1] - 1 + 127, 0) - down, 1)
    scale = np.exp2(byte - 127.0)
    codes = (blocks / scale).astype(np.float32).astype(dtype).astype(np.float64)
    return np.moveaxis((codes * scale).reshape(v.shape), -1, axis)


WIDE = False


def mx_kscale(k):
    if not WIDE:
        return np.ones(k)
    levels = np.array([10, -10, 5, -5, 0])
    if k % 512:
        return np.exp2(np.random.permutation(np.resize(levels, k // 32))).repeat(32)
    a = np.empty((k // 512, 16))
    for p in range(k // 512):
        a[p, :8] = np.random.permutation(np.resize(levels, 8))
        for g in range(8):
            far = levels[np.abs(levels - a[p, g]) >= 10]
            a[p, g + 8] = far[np.random.randint(len(far))]
    return np.exp2(a.ravel()).repeat(32)


def f64(x):
    return np.asarray(x).astype(np.float64)


def striped(idx):
    return np.tile(idx.reshape(-1, 16).T, (8, 1)).astype(np.uint16)


def unstriped(offs):
    return offs[:16].T.reshape(-1).astype(np.int64)


def pack_weight(w):
    k, n = w.shape
    w = f64(np.asarray(w, np.float32).astype(ml_dtypes.bfloat16)).reshape(k // 32, 32, n)
    amax = np.abs(w).max(1)
    byte = np.clip(np.where(amax > 0, np.frexp(amax)[1] - 1 + 127 - 7, 1), 1, 254)
    scaled = (w * np.exp2(127.0 - byte)[:, None, :]).reshape(k, n).astype(np.float32)
    words = np.ascontiguousarray(scaled.reshape(k // 512, 128, 4, n).transpose(0, 1, 3, 2)).astype(ml_dtypes.float8_e4m3fn).view(np.uint8)
    return words, np.ascontiguousarray(byte.astype(np.uint8).reshape(k // 512, 16, n))


def unpack_weight(words, scales):
    g, p, n, _ = words.shape
    vals = np.ascontiguousarray(words).view(ml_dtypes.float8_e4m3fn).astype(np.float64) * np.repeat(np.exp2(scales.astype(np.float64) - 127.0), 8, axis=1)[..., None]
    return vals.transpose(0, 1, 3, 2).reshape(g * 512, n)


def relu(v):
    return np.maximum(v, 0.0)


K, T, S, N = 512, 1024, 512, 256


def setup_inputs():
    n = np.random.standard_normal
    s = mx_kscale(K)[:, None]
    packed_xT = pack_weight(n((K, T)) * s)
    return {
        "x_words": packed_xT[0],
        "x_scales": packed_xT[1],
        "w1": (n((K, N)) / np.sqrt(K) / s).astype(np.float32),
        "w2": (n((K, N)) / np.sqrt(K) / s).astype(np.float32),
        "head": (np.random.uniform(0.4, 1.2, (N, 1))).astype(np.float32),
        "inv0": (np.random.uniform(0.4, 0.8, (N, 1))).astype(np.float32),
        "offs": striped(np.random.permutation(T)[:S]),
        "lead": striped(np.random.permutation(S)),
    }


def reference(x_words, x_scales, w1, w2, head, inv0, offs, lead):
    xq = unpack_weight(x_words, x_scales)[:, unstriped(offs)]
    y = mxq(f64(w1), 0, "e4m3").T @ xq
    spd = np.log(np.exp(y) + 1.0)
    dv = spd - spd[:, unstriped(lead)]
    ss = relu(f64(head) * spd + 0.5 * (spd * dv)) + 0.3
    z = mxq(f64(w2), 0, "e4m3").T @ xq
    gap = np.log(np.exp(z) + 1.0) + 0.5
    ac = -1.0 * (((f64(inv0) * spd) ** 2) ** 2) + 1.0 - ((ss / gap) ** 2)
    return np.maximum(ac, -2.0 * spd)

@@ -1,0 +1,166 @@
+import math
+from contextlib import ExitStack
+
+import concourse.mybir as mybir
+from concourse.masks import make_identity
+
+K, T, S, N = 512, 1024, 512, 256
+FLOPS = 2 * 2 * K * N * S
+
+F32 = mybir.dt.float32
+BF16 = mybir.dt.bfloat16
+I32 = mybir.dt.int32
+U32 = mybir.dt.uint32
+U16 = mybir.dt.uint16
+U8 = mybir.dt.uint8
+FP8X4 = mybir.dt.float8_e4m3fn_x4
+ALU = mybir.AluOpType
+ACT = mybir.ActivationFunctionType
+
+P = 128
+PACK = 4
+BLOCKS = N // P
+HALF = S // 2
+EXP_CAP = 2.0 ** 57
+LOG_CAP = 57 * math.log(2.0)
+
+
+def tile_picked_yidm_acc_p_kernel(tc, x_words, x_scales, w1, w2, head, inv0, offs, lead, out):
+    nc = tc.nc
+    with ExitStack() as ctx:
+        keep = ctx.enter_context(tc.tile_pool(name="keep", bufs=1))
+        psum = ctx.enter_context(tc.psum_pool(name="psum", bufs=1))
+
+        offs_t = keep.tile([P, S // 16], U16, name="offs_t")
+        lead_t = keep.tile([P, S // 16], U16, name="lead_t")
+        words = keep.tile([P, T], I32, name="words")
+        scales = keep.tile([P, T], U8, name="scales")
+        raw1 = keep.tile([P, PACK, N], F32, name="raw1")
+        raw2 = keep.tile([P, PACK, N], F32, name="raw2")
+        head_t = keep.tile([P, BLOCKS], F32, name="head_t")
+        inv_t = keep.tile([P, BLOCKS], F32, name="inv_t")
+        ident = keep.tile([P, P], F32, name="ident")
+
+        nc.gpsimd.memset(scales[:].bitcast(I32), 0)
+        nc.sync.dma_start(offs_t[:], offs)
+        for q in range(4):
+            nc.sync.dma_start(scales[32 * q : 32 * q + 4, :].bitcast(I32), x_scales[0, 4 * q : 4 * q + 4, :].bitcast(I32))
+        nc.sync.dma_start(raw2[:], w2.rearrange("(p j) n -> p j n", j=PACK))
+        nc.sync.dma_start(words[:], x_words[0].rearrange("p c r -> p (c r)").bitcast(I32))
+        nc.sync.dma_start(raw1[:], w1.rearrange("(p j) n -> p j n", j=PACK))
+        nc.sync.dma_start(lead_t[:], lead)
+        with nc.allow_non_contiguous_dma(reason="one value a partition and block"):
+            nc.sync.dma_start(head_t[:], head.rearrange("(b p) o -> p (b o)", p=P))
+            nc.sync.dma_start(inv_t[:], inv0.rearrange("(b p) o -> p (b o)", p=P))
+        make_identity(nc, ident[:])
+
+        picked_scales = keep.tile([P, S], U8, name="picked_scales", align_bytes=64)
+        picked_words = keep.tile([P, S], U32, name="picked_words", align_bytes=64)
+        grouped1 = [keep.tile([P, P, PACK], BF16, name=f"grouped1_{b}", align_bytes=64) for b in range(BLOCKS)]
+        codes1 = [keep.tile([P, P], U32, name=f"codes1_{b}", align_bytes=64) for b in range(BLOCKS)]
+        wscales1 = [keep.tile([P, P], U8, name=f"wscales1_{b}", align_bytes=64) for b in range(BLOCKS)]
+        grouped2 = keep.tile([P, N, PACK], BF16, name="grouped2", align_bytes=64)
+        codes2 = keep.tile([P, N], U32, name="codes2", align_bytes=64)
+        wscales2 = keep.tile([P, N], U8, name="wscales2", align_bytes=64)
+        y = [psum.tile([P, S], F32, name=f"y{b}") for b in range(BLOCKS)]
+        zt = [psum.tile([P, 2, N], F32, name=f"zt{h}") for h in range(2)]
+        gsum = [psum.tile([P, S], F32, name=f"gsum{b}") for b in range(BLOCKS)]
+
+        def cast(eng_copy, dst, raw, b):
+            eng_copy(dst.rearrange("p (c i) j -> p c j i", i=4), raw[:, :, b * P : (b + 1) * P].rearrange("p j (c i) -> p c j i", i=4))
+
+        nc.vector.tensor_copy(picked_scales[:], scales[:].indirect(offs_t[:]))
+        cast(nc.vector.tensor_copy, grouped2[:, 0:P, :], raw2, 0)
+        cast(nc.scalar.copy, grouped2[:, P:N, :], raw2, 1)
+        nc.vector.quantize_mx(out=codes2[:].bitcast(FP8X4), scales=wscales2[:], in_=grouped2[:].rearrange("p c j -> p (c j)"))
+        for h in range(2):
+            nc.vector.tensor_copy(picked_words[:, h * HALF : (h + 1) * HALF], words[:].bitcast(U32).indirect(offs_t[:, h * 16 : (h + 1) * 16]))
+            for a in range(2):
+                cols = slice((2 * h + a) * P, (2 * h + a + 1) * P)
+                nc.tensor.matmul_mx(out=zt[h][:, a, :], lhsT=picked_words[:, cols].bitcast(FP8X4), lhsT_scale=picked_scales[:, cols],
+                                    rhs=codes2[:].bitcast(FP8X4), rhs_scale=wscales2[:], start=True, stop=True)
+        for b in range(BLOCKS):
+            cast(nc.vector.tensor_copy, grouped1[b][:], raw1, b)
+            nc.vector.quantize_mx(out=codes1[b][:].bitcast(FP8X4), scales=wscales1[b][:], in_=grouped1[b][:].rearrange("p c j -> p (c j)"))
+            nc.tensor.matmul_mx(out=y[b][:], lhsT=codes1[b][:].bitcast(FP8X4), lhsT_scale=wscales1[b][:],
+                                rhs=picked_words[:].bitcast(FP8X4), rhs_scale=picked_scales[:], start=True, stop=True)
+
+        def plane(name):
+            return [keep.tile([P, S], F32, name=f"{name}{b}") for b in range(BLOCKS)]
+
+        ex = keep.tile([P, 4, S], F32, name="ex")
+        ez = [ex[:, h, :] for h in range(2)]
+        ey = [ex[:, 2 + b, :] for b in range(BLOCKS)]
+        rem, lz = plane("rem"), plane("lz")
+        for h in range(2):
+            nc.scalar.activation(ez[h], zt[h][:].rearrange("p a n -> p (a n)"), ACT.Exp)
+        for b in range(BLOCKS):
+            nc.scalar.activation(ey[b], y[b][:], ACT.Exp)
+        for h in range(2):
+            nc.vector.tensor_scalar(rem[h][:], zt[h][:].rearrange("p a n -> p (a n)"), -LOG_CAP, 0.0, ALU.add, ALU.max)
+
+        head2 = keep.tile([P, BLOCKS], F32, name="head2")
+        inv2 = keep.tile([P, BLOCKS], F32, name="inv2")
+        nc.vector.tensor_scalar(head2[:], head_t[:], 2.0, None, ALU.mult)
+        nc.vector.tensor_tensor(inv2[:], inv_t[:], inv_t[:], ALU.mult)
+        flat = ex[:].rearrange("p a s -> p (a s)")
+        nc.vector.tensor_scalar(flat, flat, EXP_CAP, None, ALU.min)
+
+        def turn(src, first):
+            for jb in range(4):
+                for b in range(BLOCKS):
+                    c0 = (jb % 2) * N + b * P
+                    nc.tensor.matmul(gsum[b][:, jb * P : (jb + 1) * P], lhsT=src[jb // 2][:, c0 : c0 + P], rhs=ident[:], is_transpose=True,
+                                     start=first and jb == 0, stop=(not first) and jb == 3)
+
+        turn(rem, True)
+
+        speed = [keep.tile([P, 2, S], F32, name=f"speed{b}") for b in range(BLOCKS)]
+        lngap, rgap = plane("lngap"), plane("rgap")
+        led, v2, h2, ss2, a2, a4, nt, ac, res = (plane(n) for n in ("led", "v2", "h2", "ss2", "a2", "a4", "nt", "ac", "res"))
+        spd = [speed[b][:, 0, :] for b in range(BLOCKS)]
+
+        def gather(b):
+            nc.vector.tensor_copy(led[b][:], speed[b][:].rearrange("p i s -> p (i s)").indirect(lead_t[:]))
+
+        def wish(b):
+            nc.vector.scalar_tensor_tensor(v2[b][:], spd[b], head2[:, b : b + 1], led[b][:], ALU.add, ALU.subtract)
+            nc.vector.scalar_tensor_tensor(h2[b][:], v2[b][:], 0.0, spd[b], ALU.max, ALU.mult)
+
+        nc.scalar.activation(speed[0][:, 1, :], ey[0], ACT.Ln, bias=1.0)
+        nc.vector.tensor_tensor(spd[0], y[0][:], speed[0][:, 1, :], ALU.max)
+        gather(0)
+        for h in range(2):
+            nc.scalar.activation(lz[h][:], ez[h], ACT.Ln, bias=1.0)
+        turn(lz, False)
+        nc.scalar.activation(speed[1][:, 1, :], ey[1], ACT.Ln, bias=1.0)
+        nc.vector.tensor_tensor(spd[1], y[1][:], speed[1][:, 1, :], ALU.max)
+        wish(0)
+        for b in range(BLOCKS):
+            nc.scalar.activation(lngap[b][:], gsum[b][:], ACT.Ln, bias=0.5)
+        nc.scalar.activation(ss2[0][:], h2[0][:], ACT.Square, bias=0.3, scale=0.5)
+        nc.scalar.activation(a2[0][:], spd[0], ACT.Square, scale=inv_t[:, 0:1])
+        gather(1)
+        wish(1)
+        nc.vector.scalar_tensor_tensor(a2[1][:], spd[1], inv2[:, 1:2], spd[1], ALU.mult, ALU.mult)
+
+        def finish(b, cols):
+            nc.vector.scalar_tensor_tensor(nt[b][:, cols], ss2[b][:, cols], -1.0, rgap[b][:, cols], ALU.mult, ALU.mult)
+
+        def finish2(b, cols):
+            nc.vector.scalar_tensor_tensor(ac[b][:, cols], nt[b][:, cols], 1.0, a4[b][:, cols], ALU.add, ALU.subtract)
+
+        def finish3(b, cols):
+            nc.vector.scalar_tensor_tensor(res[b][:, cols], spd[b][:, cols], -2.0, ac[b][:, cols], ALU.mult, ALU.max)
+            nc.sync.dma_start(out[b * P : (b + 1) * P, cols], res[b][:, cols])
+
+        halves = [slice(0, HALF), slice(HALF, S)]
+        nc.scalar.activation(rgap[0][:], lngap[0][:], ACT.Exp, scale=-2.0)
+        nc.scalar.activation(a4[0][:], a2[0][:], ACT.Square)
+        nc.scalar.activation(rgap[1][:], lngap[1][:], ACT.Exp, scale=-2.0)
+        nc.scalar.activation(ss2[1][:], h2[1][:], ACT.Square, bias=0.3, scale=0.5)
+        nc.scalar.activation(a4[1][:], a2[1][:], ACT.Square)
+        for b in range(BLOCKS):
+            for f in (finish, finish2, finish3):
+                for cols in halves:
+                    f(b, cols)

@@ -19,9 +19,14 @@ ACT = mybir.ActivationFunctionType
 
 P = 128
 PACK = 4
+QUADRANT = 32
 BLOCKS = N // P
+PIECES = S // P
 HALF = S // 2
-EXP_CAP = 2.0 ** 57
+HALVES = [slice(0, HALF), slice(HALF, S)]
+LIST_HALVES = [slice(0, HALF // 16), slice(HALF // 16, S // 16)]
+NEIGHBOURS = 4
+EXP_CAP = 2.0**57
 LOG_CAP = 57 * math.log(2.0)
 
 
@@ -31,136 +36,207 @@ def tile_picked_yidm_acc_p_kernel(tc, x_words, x_scales, w1, w2, head, inv0, off
         keep = ctx.enter_context(tc.tile_pool(name="keep", bufs=1))
         psum = ctx.enter_context(tc.psum_pool(name="psum", bufs=1))
 
+        def per_block(name):
+            return [keep.tile([P, S], F32, name=f"{name}{b}") for b in range(BLOCKS)]
+
         offs_t = keep.tile([P, S // 16], U16, name="offs_t")
         lead_t = keep.tile([P, S // 16], U16, name="lead_t")
-        words = keep.tile([P, T], I32, name="words")
-        scales = keep.tile([P, T], U8, name="scales")
-        raw1 = keep.tile([P, PACK, N], F32, name="raw1")
-        raw2 = keep.tile([P, PACK, N], F32, name="raw2")
+        table_words = keep.tile([P, T], I32, name="table_words")
+        table_scales = keep.tile([P, T], U8, name="table_scales")
+        w1_raw = keep.tile([P, PACK, N], F32, name="w1_raw")
+        w2_raw = keep.tile([P, PACK, N], F32, name="w2_raw")
         head_t = keep.tile([P, BLOCKS], F32, name="head_t")
         inv_t = keep.tile([P, BLOCKS], F32, name="inv_t")
-        ident = keep.tile([P, P], F32, name="ident")
+        identity = keep.tile([P, P], F32, name="identity")
 
-        nc.gpsimd.memset(scales[:].bitcast(I32), 0)
+        nc.vector.memset(table_scales[:].bitcast(I32), 0)
         nc.sync.dma_start(offs_t[:], offs)
-        for q in range(4):
-            nc.sync.dma_start(scales[32 * q : 32 * q + 4, :].bitcast(I32), x_scales[0, 4 * q : 4 * q + 4, :].bitcast(I32))
-        nc.sync.dma_start(raw2[:], w2.rearrange("(p j) n -> p j n", j=PACK))
-        nc.sync.dma_start(words[:], x_words[0].rearrange("p c r -> p (c r)").bitcast(I32))
-        nc.sync.dma_start(raw1[:], w1.rearrange("(p j) n -> p j n", j=PACK))
+        nc.sync.dma_start(w2_raw[:], w2.rearrange("(p t) m -> p t m", t=PACK))
+        for q in range(P // QUADRANT):
+            nc.sync.dma_start(
+                table_scales[QUADRANT * q : QUADRANT * q + 4, :].bitcast(I32),
+                x_scales[0, 4 * q : 4 * q + 4, :].bitcast(I32),
+            )
+        nc.sync.dma_start(table_words[:], x_words[0].rearrange("p c t -> p (c t)").bitcast(I32))
+        nc.sync.dma_start(w1_raw[:], w1.rearrange("(p t) m -> p t m", t=PACK))
         nc.sync.dma_start(lead_t[:], lead)
-        with nc.allow_non_contiguous_dma(reason="one value a partition and block"):
+        with nc.allow_non_contiguous_dma(reason="one value for each partition and block"):
             nc.sync.dma_start(head_t[:], head.rearrange("(b p) o -> p (b o)", p=P))
             nc.sync.dma_start(inv_t[:], inv0.rearrange("(b p) o -> p (b o)", p=P))
-        make_identity(nc, ident[:])
+        make_identity(nc, identity[:])
 
         picked_scales = keep.tile([P, S], U8, name="picked_scales", align_bytes=64)
         picked_words = keep.tile([P, S], U32, name="picked_words", align_bytes=64)
-        grouped1 = [keep.tile([P, P, PACK], BF16, name=f"grouped1_{b}", align_bytes=64) for b in range(BLOCKS)]
-        codes1 = [keep.tile([P, P], U32, name=f"codes1_{b}", align_bytes=64) for b in range(BLOCKS)]
-        wscales1 = [keep.tile([P, P], U8, name=f"wscales1_{b}", align_bytes=64) for b in range(BLOCKS)]
-        grouped2 = keep.tile([P, N, PACK], BF16, name="grouped2", align_bytes=64)
-        codes2 = keep.tile([P, N], U32, name="codes2", align_bytes=64)
-        wscales2 = keep.tile([P, N], U8, name="wscales2", align_bytes=64)
+        w1_grouped = [
+            keep.tile([P, P, PACK], BF16, name=f"w1_grouped{b}", tag=f"grouped_then_excess{b}", align_bytes=64)
+            for b in range(BLOCKS)
+        ]
+        w1_codes = [keep.tile([P, P], U32, name=f"w1_codes{b}", align_bytes=64) for b in range(BLOCKS)]
+        w1_scales = [keep.tile([P, P], U8, name=f"w1_scales{b}", align_bytes=64) for b in range(BLOCKS)]
+        w2_grouped = keep.tile([P, N, PACK], BF16, name="w2_grouped", align_bytes=64)
+        w2_codes = keep.tile([P, N], U32, name="w2_codes", align_bytes=64)
+        w2_scales = keep.tile([P, N], U8, name="w2_scales", align_bytes=64)
         y = [psum.tile([P, S], F32, name=f"y{b}") for b in range(BLOCKS)]
-        zt = [psum.tile([P, 2, N], F32, name=f"zt{h}") for h in range(2)]
-        gsum = [psum.tile([P, S], F32, name=f"gsum{b}") for b in range(BLOCKS)]
+        z_turned = [psum.tile([P, 2, N], F32, name=f"z_turned{h}") for h in range(2)]
+        gap_sum = [psum.tile([P, S], F32, name=f"gap_sum{b}") for b in range(BLOCKS)]
 
-        def cast(eng_copy, dst, raw, b):
-            eng_copy(dst.rearrange("p (c i) j -> p c j i", i=4), raw[:, :, b * P : (b + 1) * P].rearrange("p j (c i) -> p c j i", i=4))
+        def round_and_group(copy, grouped, raw, b):
+            copy(
+                grouped.rearrange("p (c i) t -> p c t i", i=NEIGHBOURS),
+                raw[:, :, b * P : (b + 1) * P].rearrange("p t (c i) -> p c t i", i=NEIGHBOURS),
+            )
 
-        nc.vector.tensor_copy(picked_scales[:], scales[:].indirect(offs_t[:]))
-        cast(nc.vector.tensor_copy, grouped2[:, 0:P, :], raw2, 0)
-        cast(nc.scalar.copy, grouped2[:, P:N, :], raw2, 1)
-        nc.vector.quantize_mx(out=codes2[:].bitcast(FP8X4), scales=wscales2[:], in_=grouped2[:].rearrange("p c j -> p (c j)"))
+        nc.vector.tensor_copy(picked_scales[:], table_scales[:].indirect(offs_t[:]))
+        for b in range(BLOCKS):
+            round_and_group(nc.scalar.copy, w2_grouped[:, b * P : (b + 1) * P, :], w2_raw, b)
+        nc.vector.quantize_mx(
+            out=w2_codes[:].bitcast(FP8X4), scales=w2_scales[:], in_=w2_grouped[:].rearrange("p m t -> p (m t)")
+        )
         for h in range(2):
-            nc.vector.tensor_copy(picked_words[:, h * HALF : (h + 1) * HALF], words[:].bitcast(U32).indirect(offs_t[:, h * 16 : (h + 1) * 16]))
+            nc.vector.tensor_copy(
+                picked_words[:, HALVES[h]], table_words[:].bitcast(U32).indirect(offs_t[:, LIST_HALVES[h]])
+            )
             for a in range(2):
-                cols = slice((2 * h + a) * P, (2 * h + a + 1) * P)
-                nc.tensor.matmul_mx(out=zt[h][:, a, :], lhsT=picked_words[:, cols].bitcast(FP8X4), lhsT_scale=picked_scales[:, cols],
-                                    rhs=codes2[:].bitcast(FP8X4), rhs_scale=wscales2[:], start=True, stop=True)
+                piece = slice((2 * h + a) * P, (2 * h + a + 1) * P)
+                nc.tensor.matmul_mx(
+                    out=z_turned[h][:, a, :],
+                    lhsT=picked_words[:, piece].bitcast(FP8X4),
+                    lhsT_scale=picked_scales[:, piece],
+                    rhs=w2_codes[:].bitcast(FP8X4),
+                    rhs_scale=w2_scales[:],
+                    start=True,
+                    stop=True,
+                )
         for b in range(BLOCKS):
-            cast(nc.vector.tensor_copy, grouped1[b][:], raw1, b)
-            nc.vector.quantize_mx(out=codes1[b][:].bitcast(FP8X4), scales=wscales1[b][:], in_=grouped1[b][:].rearrange("p c j -> p (c j)"))
-            nc.tensor.matmul_mx(out=y[b][:], lhsT=codes1[b][:].bitcast(FP8X4), lhsT_scale=wscales1[b][:],
-                                rhs=picked_words[:].bitcast(FP8X4), rhs_scale=picked_scales[:], start=True, stop=True)
+            round_and_group(nc.vector.tensor_copy, w1_grouped[b][:], w1_raw, b)
+            nc.vector.quantize_mx(
+                out=w1_codes[b][:].bitcast(FP8X4),
+                scales=w1_scales[b][:],
+                in_=w1_grouped[b][:].rearrange("p m t -> p (m t)"),
+            )
+            nc.tensor.matmul_mx(
+                out=y[b][:],
+                lhsT=w1_codes[b][:].bitcast(FP8X4),
+                lhsT_scale=w1_scales[b][:],
+                rhs=picked_words[:].bitcast(FP8X4),
+                rhs_scale=picked_scales[:],
+                start=True,
+                stop=True,
+            )
 
-        def plane(name):
-            return [keep.tile([P, S], F32, name=f"{name}{b}") for b in range(BLOCKS)]
-
-        ex = keep.tile([P, 4, S], F32, name="ex")
-        ez = [ex[:, h, :] for h in range(2)]
-        ey = [ex[:, 2 + b, :] for b in range(BLOCKS)]
-        rem, lz = plane("rem"), plane("lz")
+        exps = keep.tile([P, 2 + BLOCKS, S], F32, name="exps")
         for h in range(2):
-            nc.scalar.activation(ez[h], zt[h][:].rearrange("p a n -> p (a n)"), ACT.Exp)
+            nc.scalar.activation(exps[:, h, :], z_turned[h][:].rearrange("p a m -> p (a m)"), ACT.Exp)
         for b in range(BLOCKS):
-            nc.scalar.activation(ey[b], y[b][:], ACT.Exp)
+            nc.scalar.activation(exps[:, 2 + b, :], y[b][:], ACT.Exp)
+
+        excess = [
+            keep.tile([P, S], F32, name=f"excess{h}", tag=f"grouped_then_excess{1 - h}", align_bytes=64) for h in range(2)
+        ]
         for h in range(2):
-            nc.vector.tensor_scalar(rem[h][:], zt[h][:].rearrange("p a n -> p (a n)"), -LOG_CAP, 0.0, ALU.add, ALU.max)
+            nc.vector.tensor_scalar(
+                excess[h][:], z_turned[h][:].rearrange("p a m -> p (a m)"), -LOG_CAP, 0.0, ALU.add, ALU.max
+            )
 
-        head2 = keep.tile([P, BLOCKS], F32, name="head2")
-        inv2 = keep.tile([P, BLOCKS], F32, name="inv2")
-        nc.vector.tensor_scalar(head2[:], head_t[:], 2.0, None, ALU.mult)
-        nc.vector.tensor_tensor(inv2[:], inv_t[:], inv_t[:], ALU.mult)
-        flat = ex[:].rearrange("p a s -> p (a s)")
-        nc.vector.tensor_scalar(flat, flat, EXP_CAP, None, ALU.min)
+        all_exps = exps[:].rearrange("p r s -> p (r s)")
+        nc.vector.tensor_scalar(all_exps, all_exps, EXP_CAP, None, ALU.min)
 
-        def turn(src, first):
-            for jb in range(4):
-                for b in range(BLOCKS):
-                    c0 = (jb % 2) * N + b * P
-                    nc.tensor.matmul(gsum[b][:, jb * P : (jb + 1) * P], lhsT=src[jb // 2][:, c0 : c0 + P], rhs=ident[:], is_transpose=True,
-                                     start=first and jb == 0, stop=(not first) and jb == 3)
+        def turn_into_gap_sum(b, pieces, opens):
+            for i, piece in enumerate(pieces):
+                nc.tensor.matmul(
+                    gap_sum[b][:, i * P : (i + 1) * P],
+                    lhsT=piece,
+                    rhs=identity[:],
+                    is_transpose=True,
+                    start=opens and i == 0,
+                    stop=not opens and i == PIECES - 1,
+                )
 
-        turn(rem, True)
+        for b in range(BLOCKS):
+            starts = [(i % 2) * N + b * P for i in range(PIECES)]
+            turn_into_gap_sum(b, [excess[i // 2][:, starts[i] : starts[i] + P] for i in range(PIECES)], True)
 
         speed = [keep.tile([P, 2, S], F32, name=f"speed{b}") for b in range(BLOCKS)]
-        lngap, rgap = plane("lngap"), plane("rgap")
-        led, v2, h2, ss2, a2, a4, nt, ac, res = (plane(n) for n in ("led", "v2", "h2", "ss2", "a2", "a4", "nt", "ac", "res"))
         spd = [speed[b][:, 0, :] for b in range(BLOCKS)]
+        log_z, log_gap = per_block("log_z"), per_block("log_gap")
+        own = per_block("own")
+        closing = per_block("closing")
+        wish = per_block("wish")
+        wish_sq = per_block("wish_sq")
+        free_2 = per_block("free_2")
+        free_4 = per_block("free_4")
+        accel, result = per_block("accel"), per_block("result")
+        inv_gap_sq = [keep.tile([P, S], F32, name="inv_gap_sq0"), wish[0]]
+        ratio = [closing[1], keep.tile([P, S], F32, name="ratio1")]
 
-        def gather(b):
-            nc.vector.tensor_copy(led[b][:], speed[b][:].rearrange("p i s -> p (i s)").indirect(lead_t[:]))
+        def add_headway(b, cols):
+            headway = head_t[:, b : b + 1]
+            nc.vector.tensor_scalar(own[b][:, cols], spd[b][:, cols], headway, headway, ALU.add, ALU.add)
 
-        def wish(b):
-            nc.vector.scalar_tensor_tensor(v2[b][:], spd[b], head2[:, b : b + 1], led[b][:], ALU.add, ALU.subtract)
-            nc.vector.scalar_tensor_tensor(h2[b][:], v2[b][:], 0.0, spd[b], ALU.max, ALU.mult)
+        def gather_leaders(b):
+            window = speed[b][:].rearrange("p r s -> p (r s)")
+            for cols, entries in zip(HALVES, LIST_HALVES):
+                nc.vector.tensor_tensor(
+                    closing[b][:, cols], window.indirect(lead_t[:, entries]), own[b][:, cols], ALU.subtract
+                )
 
-        nc.scalar.activation(speed[0][:, 1, :], ey[0], ACT.Ln, bias=1.0)
-        nc.vector.tensor_tensor(spd[0], y[0][:], speed[0][:, 1, :], ALU.max)
-        gather(0)
-        for h in range(2):
-            nc.scalar.activation(lz[h][:], ez[h], ACT.Ln, bias=1.0)
-        turn(lz, False)
-        nc.scalar.activation(speed[1][:, 1, :], ey[1], ACT.Ln, bias=1.0)
+        def make_wish(b, cols):
+            nc.vector.scalar_tensor_tensor(wish[b][:, cols], closing[b][:, cols], 0.0, spd[b][:, cols], ALU.min, ALU.mult)
+
+        for cols in HALVES:
+            nc.scalar.activation(speed[0][:, 1, cols], exps[:, 2, cols], ACT.Ln, bias=1.0)
+            nc.vector.tensor_tensor(spd[0][:, cols], y[0][:, cols], speed[0][:, 1, cols], ALU.max)
+        for cols in HALVES:
+            add_headway(0, cols)
+        gather_leaders(0)
+
+        exp_z = exps[:, 0:2, :].rearrange("p h (a m) -> p (h a) m", a=2)
+        for b in range(BLOCKS):
+            for h, cols in enumerate(HALVES):
+                nc.scalar.activation(
+                    log_z[b][:, cols].rearrange("p (a c) -> p a c", a=2),
+                    exp_z[:, 2 * h : 2 * h + 2, b * P : (b + 1) * P],
+                    ACT.Ln,
+                    bias=1.0,
+                )
+            turn_into_gap_sum(b, [log_z[b][:, i * P : (i + 1) * P] for i in range(PIECES)], False)
+
+        nc.scalar.activation(speed[1][:, 1, :], exps[:, 3, :], ACT.Ln, bias=1.0)
         nc.vector.tensor_tensor(spd[1], y[1][:], speed[1][:, 1, :], ALU.max)
-        wish(0)
+        make_wish(0, slice(0, S))
         for b in range(BLOCKS):
-            nc.scalar.activation(lngap[b][:], gsum[b][:], ACT.Ln, bias=0.5)
-        nc.scalar.activation(ss2[0][:], h2[0][:], ACT.Square, bias=0.3, scale=0.5)
-        nc.scalar.activation(a2[0][:], spd[0], ACT.Square, scale=inv_t[:, 0:1])
-        gather(1)
-        wish(1)
-        nc.vector.scalar_tensor_tensor(a2[1][:], spd[1], inv2[:, 1:2], spd[1], ALU.mult, ALU.mult)
+            nc.scalar.activation(log_gap[b][:], gap_sum[b][:], ACT.Ln, bias=0.5)
+        add_headway(1, slice(0, S))
+        nc.vector.scalar_tensor_tensor(free_2[0][:], spd[0], inv_t[:, 0:1], spd[0], ALU.mult, ALU.mult)
+        gather_leaders(1)
+        for cols in HALVES:
+            make_wish(1, cols)
 
-        def finish(b, cols):
-            nc.vector.scalar_tensor_tensor(nt[b][:, cols], ss2[b][:, cols], -1.0, rgap[b][:, cols], ALU.mult, ALU.mult)
+        nc.scalar.activation(inv_gap_sq[0][:], log_gap[0][:], ACT.Exp, scale=-2.0)
+        nc.scalar.activation(wish_sq[0][:], wish[0][:], ACT.Square, bias=0.3, scale=-0.5)
+        nc.scalar.activation(free_4[0][:], free_2[0][:], ACT.Square, scale=inv_t[:, 0:1])
+        nc.scalar.activation(inv_gap_sq[1][:], log_gap[1][:], ACT.Exp, scale=-2.0)
+        nc.scalar.activation(wish_sq[1][:], wish[1][:], ACT.Square, bias=0.3, scale=-0.5)
+        for cols in HALVES:
+            nc.scalar.activation(free_2[1][:, cols], spd[1][:, cols], ACT.Square, scale=inv_t[:, 1:2])
+        for cols in HALVES:
+            nc.scalar.activation(free_4[1][:, cols], free_2[1][:, cols], ACT.Square)
 
-        def finish2(b, cols):
-            nc.vector.scalar_tensor_tensor(ac[b][:, cols], nt[b][:, cols], 1.0, a4[b][:, cols], ALU.add, ALU.subtract)
+        def finish(b, after_half):
+            for cols in HALVES:
+                nc.vector.scalar_tensor_tensor(
+                    ratio[b][:, cols], wish_sq[b][:, cols], -1.0, inv_gap_sq[b][:, cols], ALU.mult, ALU.mult
+                )
+            for cols in HALVES:
+                nc.vector.scalar_tensor_tensor(
+                    accel[b][:, cols], ratio[b][:, cols], 1.0, free_4[b][:, cols], ALU.add, ALU.subtract
+                )
+            for cols, stored in zip(HALVES, after_half):
+                nc.vector.scalar_tensor_tensor(
+                    result[b][:, cols], spd[b][:, cols], -2.0, accel[b][:, cols], ALU.mult, ALU.max
+                )
+                for part in stored:
+                    nc.sync.dma_start(out[b * P : (b + 1) * P, part], result[b][:, part])
 
-        def finish3(b, cols):
-            nc.vector.scalar_tensor_tensor(res[b][:, cols], spd[b][:, cols], -2.0, ac[b][:, cols], ALU.mult, ALU.max)
-            nc.sync.dma_start(out[b * P : (b + 1) * P, cols], res[b][:, cols])
-
-        halves = [slice(0, HALF), slice(HALF, S)]
-        nc.scalar.activation(rgap[0][:], lngap[0][:], ACT.Exp, scale=-2.0)
-        nc.scalar.activation(a4[0][:], a2[0][:], ACT.Square)
-        nc.scalar.activation(rgap[1][:], lngap[1][:], ACT.Exp, scale=-2.0)
-        nc.scalar.activation(ss2[1][:], h2[1][:], ACT.Square, bias=0.3, scale=0.5)
-        nc.scalar.activation(a4[1][:], a2[1][:], ACT.Square)
-        for b in range(BLOCKS):
-            for f in (finish, finish2, finish3):
-                for cols in halves:
-                    f(b, cols)
+        finish(0, [[], [slice(0, S)]])
+        finish(1, [[HALVES[0]], [HALVES[1]]])

import math
from contextlib import ExitStack

import concourse.mybir as mybir
from concourse.masks import make_identity

K, T, S, N = 512, 1024, 512, 256
FLOPS = 2 * 2 * K * N * S

F32 = mybir.dt.float32
BF16 = mybir.dt.bfloat16
I32 = mybir.dt.int32
U32 = mybir.dt.uint32
U16 = mybir.dt.uint16
U8 = mybir.dt.uint8
FP8X4 = mybir.dt.float8_e4m3fn_x4
ALU = mybir.AluOpType
ACT = mybir.ActivationFunctionType

P = 128
PACK = 4
QUADRANT = 32
BLOCKS = N // P
PIECES = S // P
HALF = S // 2
HALVES = [slice(0, HALF), slice(HALF, S)]
LIST_HALVES = [slice(0, HALF // 16), slice(HALF // 16, S // 16)]
NEIGHBOURS = 4
EXP_CAP = 2.0**57
LOG_CAP = 57 * math.log(2.0)


def tile_picked_yidm_acc_p_kernel(tc, x_words, x_scales, w1, w2, head, inv0, offs, lead, out):
    nc = tc.nc
    with ExitStack() as ctx:
        keep = ctx.enter_context(tc.tile_pool(name="keep", bufs=1))
        psum = ctx.enter_context(tc.psum_pool(name="psum", bufs=1))

        def per_block(name):
            return [keep.tile([P, S], F32, name=f"{name}{b}") for b in range(BLOCKS)]

        offs_t = keep.tile([P, S // 16], U16, name="offs_t")
        lead_t = keep.tile([P, S // 16], U16, name="lead_t")
        table_words = keep.tile([P, T], I32, name="table_words")
        table_scales = keep.tile([P, T], U8, name="table_scales")
        w1_raw = keep.tile([P, PACK, N], F32, name="w1_raw")
        w2_raw = keep.tile([P, PACK, N], F32, name="w2_raw")
        head_t = keep.tile([P, BLOCKS], F32, name="head_t")
        inv_t = keep.tile([P, BLOCKS], F32, name="inv_t")
        identity = keep.tile([P, P], F32, name="identity")

        nc.vector.memset(table_scales[:].bitcast(I32), 0)
        nc.sync.dma_start(offs_t[:], offs)
        nc.sync.dma_start(w2_raw[:], w2.rearrange("(p t) m -> p t m", t=PACK))
        for q in range(P // QUADRANT):
            nc.sync.dma_start(
                table_scales[QUADRANT * q : QUADRANT * q + 4, :].bitcast(I32),
                x_scales[0, 4 * q : 4 * q + 4, :].bitcast(I32),
            )
        nc.sync.dma_start(table_words[:], x_words[0].rearrange("p c t -> p (c t)").bitcast(I32))
        nc.sync.dma_start(w1_raw[:], w1.rearrange("(p t) m -> p t m", t=PACK))
        nc.sync.dma_start(lead_t[:], lead)
        with nc.allow_non_contiguous_dma(reason="one value for each partition and block"):
            nc.sync.dma_start(head_t[:], head.rearrange("(b p) o -> p (b o)", p=P))
            nc.sync.dma_start(inv_t[:], inv0.rearrange("(b p) o -> p (b o)", p=P))
        make_identity(nc, identity[:])

        picked_scales = keep.tile([P, S], U8, name="picked_scales", align_bytes=64)
        picked_words = keep.tile([P, S], U32, name="picked_words", align_bytes=64)
        w1_grouped = [
            keep.tile([P, P, PACK], BF16, name=f"w1_grouped{b}", tag=f"grouped_then_excess{b}", align_bytes=64)
            for b in range(BLOCKS)
        ]
        w1_codes = [keep.tile([P, P], U32, name=f"w1_codes{b}", align_bytes=64) for b in range(BLOCKS)]
        w1_scales = [keep.tile([P, P], U8, name=f"w1_scales{b}", align_bytes=64) for b in range(BLOCKS)]
        w2_grouped = keep.tile([P, N, PACK], BF16, name="w2_grouped", align_bytes=64)
        w2_codes = keep.tile([P, N], U32, name="w2_codes", align_bytes=64)
        w2_scales = keep.tile([P, N], U8, name="w2_scales", align_bytes=64)
        y = [psum.tile([P, S], F32, name=f"y{b}") for b in range(BLOCKS)]
        z_turned = [psum.tile([P, 2, N], F32, name=f"z_turned{h}") for h in range(2)]
        gap_sum = [psum.tile([P, S], F32, name=f"gap_sum{b}") for b in range(BLOCKS)]

        def round_and_group(copy, grouped, raw, b):
            copy(
                grouped.rearrange("p (c i) t -> p c t i", i=NEIGHBOURS),
                raw[:, :, b * P : (b + 1) * P].rearrange("p t (c i) -> p c t i", i=NEIGHBOURS),
            )

        nc.vector.tensor_copy(picked_scales[:], table_scales[:].indirect(offs_t[:]))
        for b in range(BLOCKS):
            round_and_group(nc.scalar.copy, w2_grouped[:, b * P : (b + 1) * P, :], w2_raw, b)
        nc.vector.quantize_mx(
            out=w2_codes[:].bitcast(FP8X4), scales=w2_scales[:], in_=w2_grouped[:].rearrange("p m t -> p (m t)")
        )
        for h in range(2):
            nc.vector.tensor_copy(
                picked_words[:, HALVES[h]], table_words[:].bitcast(U32).indirect(offs_t[:, LIST_HALVES[h]])
            )
            for a in range(2):
                piece = slice((2 * h + a) * P, (2 * h + a + 1) * P)
                nc.tensor.matmul_mx(
                    out=z_turned[h][:, a, :],
                    lhsT=picked_words[:, piece].bitcast(FP8X4),
                    lhsT_scale=picked_scales[:, piece],
                    rhs=w2_codes[:].bitcast(FP8X4),
                    rhs_scale=w2_scales[:],
                    start=True,
                    stop=True,
                )
        for b in range(BLOCKS):
            round_and_group(nc.vector.tensor_copy, w1_grouped[b][:], w1_raw, b)
            nc.vector.quantize_mx(
                out=w1_codes[b][:].bitcast(FP8X4),
                scales=w1_scales[b][:],
                in_=w1_grouped[b][:].rearrange("p m t -> p (m t)"),
            )
            nc.tensor.matmul_mx(
                out=y[b][:],
                lhsT=w1_codes[b][:].bitcast(FP8X4),
                lhsT_scale=w1_scales[b][:],
                rhs=picked_words[:].bitcast(FP8X4),
                rhs_scale=picked_scales[:],
                start=True,
                stop=True,
            )

        exps = keep.tile([P, 2 + BLOCKS, S], F32, name="exps")
        for h in range(2):
            nc.scalar.activation(exps[:, h, :], z_turned[h][:].rearrange("p a m -> p (a m)"), ACT.Exp)
        for b in range(BLOCKS):
            nc.scalar.activation(exps[:, 2 + b, :], y[b][:], ACT.Exp)

        excess = [
            keep.tile([P, S], F32, name=f"excess{h}", tag=f"grouped_then_excess{1 - h}", align_bytes=64) for h in range(2)
        ]
        for h in range(2):
            nc.vector.tensor_scalar(
                excess[h][:], z_turned[h][:].rearrange("p a m -> p (a m)"), -LOG_CAP, 0.0, ALU.add, ALU.max
            )

        all_exps = exps[:].rearrange("p r s -> p (r s)")
        nc.vector.tensor_scalar(all_exps, all_exps, EXP_CAP, None, ALU.min)

        def turn_into_gap_sum(b, pieces, opens):
            for i, piece in enumerate(pieces):
                nc.tensor.matmul(
                    gap_sum[b][:, i * P : (i + 1) * P],
                    lhsT=piece,
                    rhs=identity[:],
                    is_transpose=True,
                    start=opens and i == 0,
                    stop=not opens and i == PIECES - 1,
                )

        for b in range(BLOCKS):
            starts = [(i % 2) * N + b * P for i in range(PIECES)]
            turn_into_gap_sum(b, [excess[i // 2][:, starts[i] : starts[i] + P] for i in range(PIECES)], True)

        speed = [keep.tile([P, 2, S], F32, name=f"speed{b}") for b in range(BLOCKS)]
        spd = [speed[b][:, 0, :] for b in range(BLOCKS)]
        log_z, log_gap = per_block("log_z"), per_block("log_gap")
        own = per_block("own")
        closing = per_block("closing")
        wish = per_block("wish")
        wish_sq = per_block("wish_sq")
        free_2 = per_block("free_2")
        free_4 = per_block("free_4")
        accel, result = per_block("accel"), per_block("result")
        inv_gap_sq = [keep.tile([P, S], F32, name="inv_gap_sq0"), wish[0]]
        ratio = [closing[1], keep.tile([P, S], F32, name="ratio1")]

        def add_headway(b, cols):
            headway = head_t[:, b : b + 1]
            nc.vector.tensor_scalar(own[b][:, cols], spd[b][:, cols], headway, headway, ALU.add, ALU.add)

        def gather_leaders(b):
            window = speed[b][:].rearrange("p r s -> p (r s)")
            for cols, entries in zip(HALVES, LIST_HALVES):
                nc.vector.tensor_tensor(
                    closing[b][:, cols], window.indirect(lead_t[:, entries]), own[b][:, cols], ALU.subtract
                )

        def make_wish(b, cols):
            nc.vector.scalar_tensor_tensor(wish[b][:, cols], closing[b][:, cols], 0.0, spd[b][:, cols], ALU.min, ALU.mult)

        for cols in HALVES:
            nc.scalar.activation(speed[0][:, 1, cols], exps[:, 2, cols], ACT.Ln, bias=1.0)
            nc.vector.tensor_tensor(spd[0][:, cols], y[0][:, cols], speed[0][:, 1, cols], ALU.max)
        for cols in HALVES:
            add_headway(0, cols)
        gather_leaders(0)

        exp_z = exps[:, 0:2, :].rearrange("p h (a m) -> p (h a) m", a=2)
        for b in range(BLOCKS):
            for h, cols in enumerate(HALVES):
                nc.scalar.activation(
                    log_z[b][:, cols].rearrange("p (a c) -> p a c", a=2),
                    exp_z[:, 2 * h : 2 * h + 2, b * P : (b + 1) * P],
                    ACT.Ln,
                    bias=1.0,
                )
            turn_into_gap_sum(b, [log_z[b][:, i * P : (i + 1) * P] for i in range(PIECES)], False)

        nc.scalar.activation(speed[1][:, 1, :], exps[:, 3, :], ACT.Ln, bias=1.0)
        nc.vector.tensor_tensor(spd[1], y[1][:], speed[1][:, 1, :], ALU.max)
        make_wish(0, slice(0, S))
        for b in range(BLOCKS):
            nc.scalar.activation(log_gap[b][:], gap_sum[b][:], ACT.Ln, bias=0.5)
        add_headway(1, slice(0, S))
        nc.vector.scalar_tensor_tensor(free_2[0][:], spd[0], inv_t[:, 0:1], spd[0], ALU.mult, ALU.mult)
        gather_leaders(1)
        for cols in HALVES:
            make_wish(1, cols)

        nc.scalar.activation(inv_gap_sq[0][:], log_gap[0][:], ACT.Exp, scale=-2.0)
        nc.scalar.activation(wish_sq[0][:], wish[0][:], ACT.Square, bias=0.3, scale=-0.5)
        nc.scalar.activation(free_4[0][:], free_2[0][:], ACT.Square, scale=inv_t[:, 0:1])
        nc.scalar.activation(inv_gap_sq[1][:], log_gap[1][:], ACT.Exp, scale=-2.0)
        nc.scalar.activation(wish_sq[1][:], wish[1][:], ACT.Square, bias=0.3, scale=-0.5)
        for cols in HALVES:
            nc.scalar.activation(free_2[1][:, cols], spd[1][:, cols], ACT.Square, scale=inv_t[:, 1:2])
        for cols in HALVES:
            nc.scalar.activation(free_4[1][:, cols], free_2[1][:, cols], ACT.Square)

        def finish(b, after_half):
            for cols in HALVES:
                nc.vector.scalar_tensor_tensor(
                    ratio[b][:, cols], wish_sq[b][:, cols], -1.0, inv_gap_sq[b][:, cols], ALU.mult, ALU.mult
                )
            for cols in HALVES:
                nc.vector.scalar_tensor_tensor(
                    accel[b][:, cols], ratio[b][:, cols], 1.0, free_4[b][:, cols], ALU.add, ALU.subtract
                )
            for cols, stored in zip(HALVES, after_half):
                nc.vector.scalar_tensor_tensor(
                    result[b][:, cols], spd[b][:, cols], -2.0, accel[b][:, cols], ALU.mult, ALU.max
                )
                for part in stored:
                    nc.sync.dma_start(out[b * P : (b + 1) * P, part], result[b][:, part])

        finish(0, [[], [slice(0, S)]])
        finish(1, [[HALVES[0]], [HALVES[1]]])
